import numpy as np
import ml_dtypes


def mxq(x, axis, fmt="e4m3"):
    dtype, down = {"e4m3": (ml_dtypes.float8_e4m3fn, 7), "e5m2": (ml_dtypes.float8_e5m2, 14)}[fmt]
    v = np.moveaxis(np.asarray(x, np.float32).astype(ml_dtypes.bfloat16).astype(np.float64), axis, -1)
    blocks = v.reshape(v.shape[:-1] + (-1, 32))
    amax = np.abs(blocks).max(-1, keepdims=True)
    byte = np.maximum(np.where(amax > 0, np.frexp(amax)[1] - 1 + 127, 0) - down, 1)
    scale = np.exp2(byte - 127.0)
    codes = (blocks / scale).astype(np.float32).astype(dtype).astype(np.float64)
    return np.moveaxis((codes * scale).reshape(v.shape), -1, axis)


WIDE = False


def mx_kscale(k):
    if not WIDE:
        return np.ones(k)
    levels = np.array([24, -24, 12, -12, 0])
    if k % 512:
        return np.exp2(np.random.permutation(np.resize(levels, k // 32))).repeat(32)
    a = np.empty((k // 512, 16))
    for p in range(k // 512):
        a[p, :8] = np.random.permutation(np.resize(levels, 8))
        for g in range(8):
            far = levels[np.abs(levels - a[p, g]) >= 10]
            a[p, g + 8] = far[np.random.randint(len(far))]
    return np.exp2(a.ravel()).repeat(32)


def f64(x):
    return np.asarray(x).astype(np.float64)


def striped(idx):
    return np.tile(idx.reshape(-1, 16).T, (8, 1)).astype(np.uint16)


def unstriped(offs):
    return offs[:16].T.reshape(-1).astype(np.int64)


E2M1 = np.array([0.0, 0.5, 1.0, 1.5, 2.0, 3.0, 4.0, 6.0, -0.0, -0.5, -1.0, -1.5, -2.0, -3.0, -4.0, -6.0])


def pack_weight(w, fmt):
    k, n = w.shape
    w = f64(np.asarray(w, np.float32).astype(ml_dtypes.bfloat16)).reshape(k // 32, 32, n)
    amax = np.abs(w).max(1)
    if fmt == "e4m3":
        byte = np.frexp(amax)[1] - 1 + 127 - 7
    else:
        mant, ex = np.frexp(amax / 6.0)
        byte = np.where(mant > 0.5, ex, ex - 1) + 127
    byte = np.clip(np.where(amax > 0, byte, 1), 1, 254)
    scaled = (w * np.exp2(127.0 - byte)[:, None, :]).reshape(k, n).astype(np.float32)
    by_word = np.ascontiguousarray(scaled.reshape(k // 512, 128, 4, n).transpose(0, 1, 3, 2))
    if fmt == "e4m3":
        words = by_word.astype(ml_dtypes.float8_e4m3fn).view(np.uint8)
    else:
        c = by_word.astype(ml_dtypes.float4_e2m1fn).view(np.uint8) & 0xF
        words = (c[..., 0::2] | (c[..., 1::2] << 4)).reshape(k // 512, 128, 2 * n)
    return np.ascontiguousarray(words), np.ascontiguousarray(byte.astype(np.uint8).reshape(k // 512, 16, n))


def unpack_weight(words, scales, fmt):
    g, _, n = scales.shape
    words = np.ascontiguousarray(words).reshape(g, 128, n, -1)
    if fmt == "e4m3":
        vals = words.view(ml_dtypes.float8_e4m3fn).astype(np.float64)
    else:
        nib = np.empty((g, 128, n, 4), np.uint8)
        nib[..., 0::2] = words & 0xF
        nib[..., 1::2] = words >> 4
        vals = E2M1[nib]
    vals = vals * np.repeat(np.exp2(scales.astype(np.float64) - 127.0), 8, axis=1)[..., None]
    return vals.transpose(0, 1, 3, 2).reshape(g * 512, n)


def sigm(f):
    return 1.0 / (1.0 + np.exp(-np.maximum(f, -700.0)))


K, N, T, J = 1024, 512, 2048, 1024


def setup_inputs():
    n = np.random.standard_normal
    s = mx_kscale(K)[:, None]
    p_tab = pack_weight(n((K, T)) * s, "e4m3")
    return {
        "tab_words": p_tab[0],
        "tab_scales": p_tab[1],
        "wk": (n((K, N)) / np.sqrt(K) / s).astype(np.float32),
        "wv": (n((K, N)) / np.sqrt(K) / s).astype(np.float32),
        "st": (n((N, J))).astype(np.float32),
        "b": (0.3 * n(N)).astype(np.float32),
        "res": (n((N, J))).astype(np.float32),
        "offs": striped(np.random.permutation(T)[:J]),
    }


def reference(tab_words, tab_scales, wk, wv, st, b, res, offs):
    idx = unstriped(offs)
    tab_ = unpack_weight(tab_words, tab_scales, "e4m3")[:, idx]
    wk_ = mxq(f64(wk), 0, "e4m3")
    wv_q_ = mxq(f64(wv), 0, "e4m3")
    wv_r_ = mxq(f64(wv) - wv_q_, 0, "e4m3")
    ke = wk_.T @ tab_
    ve = wv_q_.T @ tab_ + wv_r_.T @ tab_
    gate = sigm(ke * f64(st) + f64(b)[:, None])
    return f64(res) + gate * ve

@@ -1,0 +1,224 @@
+from contextlib import ExitStack
+
+import concourse.mybir as mybir
+
+K, N, T, J = 1024, 512, 2048, 1024
+FLOPS = 3758096384
+
+F32 = mybir.dt.float32
+BF16 = mybir.dt.bfloat16
+I32 = mybir.dt.int32
+U32 = mybir.dt.uint32
+U16 = mybir.dt.uint16
+U8 = mybir.dt.uint8
+FP8X4 = mybir.dt.float8_e4m3fn_x4
+ALU = mybir.AluOpType
+ACT = mybir.ActivationFunctionType
+
+P = 128
+PACK = 4
+PASSES = K // (P * PACK)
+HALF = N // 2
+JT = 512
+VE_BANKS = 5
+AUX_BANKS = 3
+POOL_ADDS = 6
+
+
+def tile_list_engram_tier_bsig_kernel(
+    tc, tab_words, tab_scales, wk, wv, st, b, res, offs, out
+):
+    nc = tc.nc
+    with ExitStack() as ctx:
+        keep = ctx.enter_context(tc.tile_pool(name="keep", bufs=1))
+        work = ctx.enter_context(tc.tile_pool(name="work", bufs=8))
+        psum = ctx.enter_context(tc.psum_pool(name="psum", bufs=1))
+
+        def load_words(a):
+            t = keep.tile([P, T], I32, name=f"words{a}", align_bytes=64)
+            nc.sync.dma_start(out=t[:], in_=tab_words[a].rearrange("p t i -> p (t i)").bitcast(I32))
+            return t
+
+        def load_weight(w, a, name):
+            t = keep.tile([P, PACK, N], F32, name=name, align_bytes=64)
+            rows = w[a * P * PACK : (a + 1) * P * PACK, :]
+            nc.sync.dma_start(out=t[:], in_=rows.rearrange("(p j) n -> p j n", j=PACK))
+            return t
+
+        def load_rows(x, c, name):
+            t = keep.tile([P, J], F32, name=name, align_bytes=64)
+            nc.sync.dma_start(out=t[:], in_=x[c * P : (c + 1) * P, :])
+            return t
+
+        scale_win = keep.tile([P, T // 4], I32, name="scale_win", align_bytes=64)
+        nc.vector.memset(scale_win[:], 0)
+        eye = keep.tile([P, PACK * P * PACK], BF16, name="eye", align_bytes=64)
+        nc.vector.memset(eye[:], 0.0)
+
+        words = [load_words(0)]
+        offsets = keep.tile([P, J // 16], U16, name="offsets")
+        nc.sync.dma_start(offsets[:], offs)
+        words.append(load_words(1))
+        for q in range(4):
+            nc.sync.dma_start(
+                out=scale_win[32 * q : 32 * q + 4 * PASSES, :],
+                in_=tab_scales[:, 4 * q : 4 * q + 4, :].bitcast(I32),
+            )
+        wv_raw = [load_weight(wv, a, f"wv_raw{a}") for a in range(PASSES)]
+        wk_raw = [load_weight(wk, a, f"wk_raw{a}") for a in range(PASSES)]
+        bias = keep.tile([P, N // P], F32, name="bias")
+        with nc.allow_non_contiguous_dma(reason="one bias value a partition"):
+            nc.sync.dma_start(out=bias[:], in_=b.rearrange("(c p) -> p c", p=P))
+        st_sb, res_sb = [], []
+        for c in range(N // P):
+            st_sb.append(load_rows(st, c, f"st{c}"))
+            res_sb.append(load_rows(res, c, f"res{c}"))
+
+        nc.gpsimd.affine_select(
+            out=eye[:],
+            in_=eye[:],
+            compare_op=ALU.not_equal,
+            fill=1.0,
+            base=0,
+            pattern=[[-1, PACK], [PACK, P], [1, PACK]],
+            channel_multiplier=-PACK,
+        )
+
+        def quantize(src, name):
+            width = src.shape[1] // PACK
+            codes = keep.tile([P, width], U32, name=name + "_c", align_bytes=64)
+            scales = keep.tile([P, width], U8, name=name + "_s", align_bytes=64)
+            nc.vector.quantize_mx(out=codes[:].bitcast(FP8X4), scales=scales[:], in_=src)
+            return codes, scales
+
+        eye_q = quantize(eye[:], "eye")
+
+        picked = []
+        for a in range(PASSES):
+            g = keep.tile([P, J], U32, name=f"picked{a}", align_bytes=64)
+            nc.vector.tensor_copy(g[:], words[a][:].bitcast(U32).indirect(offsets[:]))
+            picked.append(g)
+        picked_s = keep.tile([P, J], U8, name="picked_s", align_bytes=64)
+        nc.vector.tensor_copy(picked_s[:], scale_win[:].bitcast(U8).indirect(offsets[:]))
+
+        def by_fours_out(t):
+            return t.rearrange("p (c i t) -> p c t i", i=4, t=PACK)
+
+        def by_fours_in(t):
+            return t.rearrange("p t (c i) -> p c t i", i=4)
+
+        def cast(raw, n0, n1, name):
+            g = keep.tile([P, (n1 - n0) * PACK], BF16, name=name, align_bytes=64)
+            nc.scalar.copy(out=by_fours_out(g[:]), in_=by_fours_in(raw[:, :, n0:n1]))
+            return g
+
+        units = [(a, h) for a in range(PASSES) for h in range(2)]
+        wv_bf = [cast(wv_raw[a], h * HALF, (h + 1) * HALF, f"wv_bf{a}{h}") for a, h in units]
+        wk_bf0 = cast(wk_raw[0], 0, N, "wk_bf0")
+        wk_bf1 = [cast(wk_raw[1], h * HALF, (h + 1) * HALF, f"wk_bf1{h}") for h in range(2)]
+
+        wv_q, wv_r, left = {}, {}, {}
+
+        def quantize_hi(u):
+            wv_q[u] = quantize(wv_bf[u][:], f"wv_q{u}")
+            left[u] = keep.tile([P, HALF * PACK], BF16, name=f"left{u}", align_bytes=64)
+
+        def leftover(u, cc):
+            a, h = units[u]
+            bank = psum.tile([P, PACK, P], F32, name="aux", tag="aux", bufs=AUX_BANKS)
+            cols = slice(cc * P, (cc + 1) * P)
+            for t in range(PACK):
+                nc.tensor.matmul_mx(
+                    out=bank[:, t, :],
+                    lhsT=eye_q[0][:, t * P : (t + 1) * P].bitcast(FP8X4),
+                    lhsT_scale=eye_q[1][:, t * P : (t + 1) * P],
+                    rhs=wv_q[u][0][:, cols].bitcast(FP8X4),
+                    rhs_scale=wv_q[u][1][:, cols],
+                    start=True,
+                    stop=True,
+                )
+            n0 = h * HALF + cc * P
+            nc.vector.tensor_tensor(
+                out=by_fours_out(left[u][:, cc * P * PACK : (cc + 1) * P * PACK]),
+                in0=by_fours_in(wv_raw[a][:, :, n0 : n0 + P]),
+                in1=by_fours_in(bank[:]),
+                op=ALU.subtract,
+            )
+
+        def quantize_lo(u):
+            wv_r[u] = quantize(left[u][:], f"wv_r{u}")
+
+        quantize_hi(0)
+        quantize_hi(1)
+        leftover(0, 0)
+        leftover(0, 1)
+        quantize_hi(2)
+        leftover(1, 0)
+        quantize_lo(0)
+        leftover(1, 1)
+        quantize_hi(3)
+        leftover(2, 0)
+        quantize_lo(1)
+        leftover(2, 1)
+        wk_q0 = quantize(wk_bf0[:], "wk_q0")
+        leftover(3, 0)
+        quantize_lo(2)
+        leftover(3, 1)
+        wk_q1 = [quantize(wk_bf1[0][:], "wk_q10")]
+        quantize_lo(3)
+        wk_q1.append(quantize(wk_bf1[1][:], "wk_q11"))
+
+        def product(bank, parts, jh):
+            js = slice(jh * JT, (jh + 1) * JT)
+            for i, (pair, m0, a) in enumerate(parts):
+                nc.tensor.matmul_mx(
+                    out=bank[:],
+                    lhsT=pair[0][:, m0 : m0 + P].bitcast(FP8X4),
+                    lhsT_scale=pair[1][:, m0 : m0 + P],
+                    rhs=picked[a][:, js].bitcast(FP8X4),
+                    rhs_scale=picked_s[4 * a :, js],
+                    start=(i == 0),
+                    stop=(i == len(parts) - 1),
+                )
+
+        tiles = [(c, jh) for c in range(N // P) for jh in range(J // JT)]
+        ve, gate = {}, {}
+
+        def value(i):
+            c, jh = tiles[i]
+            h, m0 = c // 2, (c % 2) * P
+            ve[i] = psum.tile([P, JT], F32, name="ve", tag="ve", bufs=VE_BANKS)
+            parts = [(wv_q[h], m0, 0), (wv_r[h], m0, 0), (wv_q[2 + h], m0, 1), (wv_r[2 + h], m0, 1)]
+            product(ve[i], parts, jh)
+
+        def make_gate(i):
+            c, jh = tiles[i]
+            h, m0 = c // 2, (c % 2) * P
+            ke = psum.tile([P, JT], F32, name="aux", tag="aux", bufs=AUX_BANKS)
+            product(ke, [(wk_q0, c * P, 0), (wk_q1[h], m0, 1)], jh)
+            logit = work.tile([P, JT], F32, name="logit")
+            nc.vector.tensor_tensor(
+                out=logit[:], in0=st_sb[c][:, jh * JT : (jh + 1) * JT], in1=ke[:], op=ALU.mult
+            )
+            gate[i] = work.tile([P, JT], F32, name="gate")
+            nc.scalar.activation(out=gate[i][:], in_=logit[:], func=ACT.Sigmoid, bias=bias[:, c : c + 1])
+
+        def finish(i):
+            c, jh = tiles[i]
+            js = slice(jh * JT, (jh + 1) * JT)
+            gated = work.tile([P, JT], F32, name="gated")
+            nc.vector.tensor_tensor(out=gated[:], in0=gate[i][:], in1=ve[i][:], op=ALU.mult)
+            result = keep.tile([P, JT], F32, name=f"result{i}")
+            adder = nc.gpsimd if i < POOL_ADDS else nc.vector
+            adder.tensor_tensor(out=result[:], in0=gated[:], in1=res_sb[c][:, js], op=ALU.add)
+            nc.sync.dma_start(out=out[c * P : (c + 1) * P, js], in_=result[:])
+
+        for i in range(VE_BANKS):
+            value(i)
+        make_gate(0)
+        for i in range(len(tiles)):
+            if i + 1 < len(tiles):
+                make_gate(i + 1)
+            finish(i)
+            if i + VE_BANKS < len(tiles):
+                value(i + VE_BANKS)

@@ -1,6 +1,7 @@
 from contextlib import ExitStack
 
 import concourse.mybir as mybir
+from concourse.masks import make_identity
 
 K, N, T, J = 1024, 512, 2048, 1024
 FLOPS = 3758096384
@@ -35,7 +36,7 @@ def tile_list_engram_tier_bsig_kernel(
         psum = ctx.enter_context(tc.psum_pool(name="psum", bufs=1))
 
         def load_words(a):
-            t = keep.tile([P, T], I32, name=f"words{a}", align_bytes=64)
+            t = keep.tile([P, T], I32, name=f"words{a}", tag=f"words{a}", align_bytes=64)
             nc.sync.dma_start(out=t[:], in_=tab_words[a].rearrange("p t i -> p (t i)").bitcast(I32))
             return t
 
@@ -50,54 +51,57 @@ def tile_list_engram_tier_bsig_kernel(
             nc.sync.dma_start(out=t[:], in_=x[c * P : (c + 1) * P, :])
             return t
 
-        scale_win = keep.tile([P, T // 4], I32, name="scale_win", align_bytes=64)
+        scale_win = keep.tile([P, T // 4], I32, name="scale_win", tag="scale_win", align_bytes=64)
         nc.vector.memset(scale_win[:], 0)
-        eye = keep.tile([P, PACK * P * PACK], BF16, name="eye", align_bytes=64)
-        nc.vector.memset(eye[:], 0.0)
+        eye = keep.tile([P, PACK, P * PACK + 1], BF16, name="eye", align_bytes=64)
+        eye_flat = eye[:].rearrange("p t x -> p (t x)")
+        nc.vector.memset(eye_flat, 0.0)
+        ident = keep.tile([P, P], F32, name="ident")
+        make_identity(nc, ident[:])
+        nc.vector.tensor_copy(
+            out=eye[:, :, 0 : P * PACK : PACK], in_=ident[:].unsqueeze(1).to_broadcast([P, PACK, P])
+        )
 
         words = [load_words(0)]
         offsets = keep.tile([P, J // 16], U16, name="offsets")
         nc.sync.dma_start(offsets[:], offs)
-        words.append(load_words(1))
         for q in range(4):
             nc.sync.dma_start(
                 out=scale_win[32 * q : 32 * q + 4 * PASSES, :],
                 in_=tab_scales[:, 4 * q : 4 * q + 4, :].bitcast(I32),
             )
-        wv_raw = [load_weight(wv, a, f"wv_raw{a}") for a in range(PASSES)]
+        wv_raw = [load_weight(wv, 0, "wv_raw0")]
+        words.append(load_words(1))
+        wv_raw.append(load_weight(wv, 1, "wv_raw1"))
         wk_raw = [load_weight(wk, a, f"wk_raw{a}") for a in range(PASSES)]
+        bias_rows = keep.tile([P, P], F32, name="bias_rows")
+        nc.gpsimd.memset(bias_rows[:], 0.0)
+        nc.gpsimd.dma_start(out=bias_rows[0 : N // P, :], in_=b.rearrange("(c p) -> c p", p=P))
+        bias_bank = psum.tile([P, P], F32, name="aux", tag="aux", bufs=AUX_BANKS)
+        nc.tensor.transpose(bias_bank[:], bias_rows[:], ident[:])
         bias = keep.tile([P, N // P], F32, name="bias")
-        with nc.allow_non_contiguous_dma(reason="one bias value a partition"):
-            nc.sync.dma_start(out=bias[:], in_=b.rearrange("(c p) -> p c", p=P))
+        nc.scalar.copy(out=bias[:], in_=bias_bank[:, 0 : N // P])
         st_sb, res_sb = [], []
         for c in range(N // P):
             st_sb.append(load_rows(st, c, f"st{c}"))
             res_sb.append(load_rows(res, c, f"res{c}"))
 
-        nc.gpsimd.affine_select(
-            out=eye[:],
-            in_=eye[:],
-            compare_op=ALU.not_equal,
-            fill=1.0,
-            base=0,
-            pattern=[[-1, PACK], [PACK, P], [1, PACK]],
-            channel_multiplier=-PACK,
-        )
-
-        def quantize(src, name):
+        def quantize(src, name, slot):
             width = src.shape[1] // PACK
-            codes = keep.tile([P, width], U32, name=name + "_c", align_bytes=64)
+            codes = keep.tile([P, width], U32, name=name + "_c", tag=slot, align_bytes=64)
             scales = keep.tile([P, width], U8, name=name + "_s", align_bytes=64)
             nc.vector.quantize_mx(out=codes[:].bitcast(FP8X4), scales=scales[:], in_=src)
             return codes, scales
 
-        eye_q = quantize(eye[:], "eye")
+        eye_q = quantize(eye_flat[:, 0 : PACK * P * PACK], "eye_q", "eye_c")
 
-        picked = []
-        for a in range(PASSES):
-            g = keep.tile([P, J], U32, name=f"picked{a}", align_bytes=64)
-            nc.vector.tensor_copy(g[:], words[a][:].bitcast(U32).indirect(offsets[:]))
-            picked.append(g)
+        picked = {}
+
+        def pick_words(a, slot):
+            picked[a] = keep.tile([P, J], U32, name=f"picked{a}", tag=slot, align_bytes=64)
+            nc.vector.tensor_copy(picked[a][:], words[a][:].bitcast(U32).indirect(offsets[:]))
+
+        pick_words(0, "picked0")
         picked_s = keep.tile([P, J], U8, name="picked_s", align_bytes=64)
         nc.vector.tensor_copy(picked_s[:], scale_win[:].bitcast(U8).indirect(offsets[:]))
 
@@ -108,7 +112,7 @@ def tile_list_engram_tier_bsig_kernel(
             return t.rearrange("p t (c i) -> p c t i", i=4)
 
         def cast(raw, n0, n1, name):
-            g = keep.tile([P, (n1 - n0) * PACK], BF16, name=name, align_bytes=64)
+            g = keep.tile([P, (n1 - n0) * PACK], BF16, name=name, tag=name, align_bytes=64)
             nc.scalar.copy(out=by_fours_out(g[:]), in_=by_fours_in(raw[:, :, n0:n1]))
             return g
 
@@ -119,9 +123,9 @@ def tile_list_engram_tier_bsig_kernel(
 
         wv_q, wv_r, left = {}, {}, {}
 
-        def quantize_hi(u):
-            wv_q[u] = quantize(wv_bf[u][:], f"wv_q{u}")
-            left[u] = keep.tile([P, HALF * PACK], BF16, name=f"left{u}", align_bytes=64)
+        def quantize_hi(u, slot):
+            wv_q[u] = quantize(wv_bf[u][:], f"wv_q{u}", slot)
+            left[u] = keep.tile([P, HALF * PACK], BF16, name=f"left{u}", tag=f"left{u}", align_bytes=64)
 
         def leftover(u, cc):
             a, h = units[u]
@@ -146,27 +150,28 @@ def tile_list_engram_tier_bsig_kernel(
             )
 
         def quantize_lo(u):
-            wv_r[u] = quantize(left[u][:], f"wv_r{u}")
+            wv_r[u] = quantize(left[u][:], f"wv_r{u}", f"wv_r{u}")
 
-        quantize_hi(0)
-        quantize_hi(1)
+        quantize_hi(0, "scale_win")
+        quantize_hi(1, "wv_q1")
+        pick_words(1, "wv_bf01")
         leftover(0, 0)
+        quantize_hi(2, "words1")
         leftover(0, 1)
-        quantize_hi(2)
         leftover(1, 0)
         quantize_lo(0)
         leftover(1, 1)
-        quantize_hi(3)
+        quantize_hi(3, "left0")
         leftover(2, 0)
         quantize_lo(1)
         leftover(2, 1)
-        wk_q0 = quantize(wk_bf0[:], "wk_q0")
+        wk_q0 = quantize(wk_bf0[:], "wk_q0", "left1")
         leftover(3, 0)
         quantize_lo(2)
         leftover(3, 1)
-        wk_q1 = [quantize(wk_bf1[0][:], "wk_q10")]
+        wk_q1 = [quantize(wk_bf1[0][:], "wk_q10", "left2")]
         quantize_lo(3)
-        wk_q1.append(quantize(wk_bf1[1][:], "wk_q11"))
+        wk_q1.append(quantize(wk_bf1[1][:], "wk_q11", "left3"))
 
         def product(bank, parts, jh):
             js = slice(jh * JT, (jh + 1) * JT)

@@ -23,7 +23,7 @@ HALF = N // 2
 JT = 512
 VE_BANKS = 5
 AUX_BANKS = 3
-POOL_ADDS = 6
+POOL_ADDS = 5
 
 
 def tile_list_engram_tier_bsig_kernel(
@@ -53,14 +53,16 @@ def tile_list_engram_tier_bsig_kernel(
 
         scale_win = keep.tile([P, T // 4], I32, name="scale_win", tag="scale_win", align_bytes=64)
         nc.vector.memset(scale_win[:], 0)
-        eye = keep.tile([P, PACK, P * PACK + 1], BF16, name="eye", align_bytes=64)
-        eye_flat = eye[:].rearrange("p t x -> p (t x)")
-        nc.vector.memset(eye_flat, 0.0)
-        ident = keep.tile([P, P], F32, name="ident")
-        make_identity(nc, ident[:])
-        nc.vector.tensor_copy(
-            out=eye[:, :, 0 : P * PACK : PACK], in_=ident[:].unsqueeze(1).to_broadcast([P, PACK, P])
-        )
+        bias_rows = keep.tile([P, P], F32, name="bias_rows")
+        nc.gpsimd.memset(bias_rows[:], 0.0)
+        strip = keep.tile([P, (2 * PACK - 1) * P], F32, name="strip", align_bytes=64)
+        nc.gpsimd.memset(strip[:], 0.0)
+        ident = strip[:, (PACK - 1) * P : PACK * P]
+        make_identity(nc, ident, nomemset=True)
+        eye = keep.tile([P, PACK, P, PACK], BF16, name="eye", tag="eye", align_bytes=64)
+        for t in range(PACK):
+            shifted = strip[:, (PACK - 1 - t) * P : (2 * PACK - 1 - t) * P]
+            nc.vector.tensor_copy(out=eye[:, t, :, :], in_=shifted.rearrange("p (i m) -> p m i", i=PACK))
 
         words = [load_words(0)]
         offsets = keep.tile([P, J // 16], U16, name="offsets")
@@ -70,15 +72,13 @@ def tile_list_engram_tier_bsig_kernel(
                 out=scale_win[32 * q : 32 * q + 4 * PASSES, :],
                 in_=tab_scales[:, 4 * q : 4 * q + 4, :].bitcast(I32),
             )
+        nc.sync.dma_start(out=bias_rows[0 : N // P, :], in_=b.rearrange("(c p) -> c p", p=P))
         wv_raw = [load_weight(wv, 0, "wv_raw0")]
         words.append(load_words(1))
         wv_raw.append(load_weight(wv, 1, "wv_raw1"))
         wk_raw = [load_weight(wk, a, f"wk_raw{a}") for a in range(PASSES)]
-        bias_rows = keep.tile([P, P], F32, name="bias_rows")
-        nc.gpsimd.memset(bias_rows[:], 0.0)
-        nc.gpsimd.dma_start(out=bias_rows[0 : N // P, :], in_=b.rearrange("(c p) -> c p", p=P))
         bias_bank = psum.tile([P, P], F32, name="aux", tag="aux", bufs=AUX_BANKS)
-        nc.tensor.transpose(bias_bank[:], bias_rows[:], ident[:])
+        nc.tensor.transpose(bias_bank[:], bias_rows[:], ident)
         bias = keep.tile([P, N // P], F32, name="bias")
         nc.scalar.copy(out=bias[:], in_=bias_bank[:, 0 : N // P])
         st_sb, res_sb = [], []
@@ -93,7 +93,7 @@ def tile_list_engram_tier_bsig_kernel(
             nc.vector.quantize_mx(out=codes[:].bitcast(FP8X4), scales=scales[:], in_=src)
             return codes, scales
 
-        eye_q = quantize(eye_flat[:, 0 : PACK * P * PACK], "eye_q", "eye_c")
+        eye_q = quantize(eye[:].rearrange("p t m i -> p (t m i)"), "eye_q", "eye_c")
 
         picked = {}
 
@@ -101,8 +101,8 @@ def tile_list_engram_tier_bsig_kernel(
             picked[a] = keep.tile([P, J], U32, name=f"picked{a}", tag=slot, align_bytes=64)
             nc.vector.tensor_copy(picked[a][:], words[a][:].bitcast(U32).indirect(offsets[:]))
 
-        pick_words(0, "picked0")
-        picked_s = keep.tile([P, J], U8, name="picked_s", align_bytes=64)
+        pick_words(0, "eye")
+        picked_s = keep.tile([P, J], U8, name="picked_s", tag="words0", align_bytes=64)
         nc.vector.tensor_copy(picked_s[:], scale_win[:].bitcast(U8).indirect(offsets[:]))
 
         def by_fours_out(t):
@@ -156,9 +156,9 @@ def tile_list_engram_tier_bsig_kernel(
         quantize_hi(1, "wv_q1")
         pick_words(1, "wv_bf01")
         leftover(0, 0)
-        quantize_hi(2, "words1")
         leftover(0, 1)
         leftover(1, 0)
+        quantize_hi(2, "words1")
         quantize_lo(0)
         leftover(1, 1)
         quantize_hi(3, "left0")
@@ -187,7 +187,7 @@ def tile_list_engram_tier_bsig_kernel(
                 )
 
         tiles = [(c, jh) for c in range(N // P) for jh in range(J // JT)]
-        ve, gate = {}, {}
+        ve, gate, gated = {}, {}, {}
 
         def value(i):
             c, jh = tiles[i]
@@ -205,25 +205,32 @@ def tile_list_engram_tier_bsig_kernel(
             nc.vector.tensor_tensor(
                 out=logit[:], in0=st_sb[c][:, jh * JT : (jh + 1) * JT], in1=ke[:], op=ALU.mult
             )
-            gate[i] = work.tile([P, JT], F32, name="gate")
+            gate[i] = keep.tile([P, JT], F32, name=f"gate{i}", tag=f"gate{i}")
             nc.scalar.activation(out=gate[i][:], in_=logit[:], func=ACT.Sigmoid, bias=bias[:, c : c + 1])
 
-        def finish(i):
+        def apply_gate(i):
+            gated[i] = work.tile([P, JT], F32, name="gated")
+            nc.vector.tensor_tensor(out=gated[i][:], in0=gate[i][:], in1=ve[i][:], op=ALU.mult)
+
+        def finish(i, adder, slot):
             c, jh = tiles[i]
             js = slice(jh * JT, (jh + 1) * JT)
-            gated = work.tile([P, JT], F32, name="gated")
-            nc.vector.tensor_tensor(out=gated[:], in0=gate[i][:], in1=ve[i][:], op=ALU.mult)
-            result = keep.tile([P, JT], F32, name=f"result{i}")
-            adder = nc.gpsimd if i < POOL_ADDS else nc.vector
-            adder.tensor_tensor(out=result[:], in0=gated[:], in1=res_sb[c][:, js], op=ALU.add)
+            result = keep.tile([P, JT], F32, name=f"result{i}", tag=slot)
+            adder.tensor_tensor(out=result[:], in0=gated[i][:], in1=res_sb[c][:, js], op=ALU.add)
             nc.sync.dma_start(out=out[c * P : (c + 1) * P, js], in_=result[:])
 
+        last = len(tiles) - 1
         for i in range(VE_BANKS):
             value(i)
         make_gate(0)
         for i in range(len(tiles)):
-            if i + 1 < len(tiles):
+            if i < last:
                 make_gate(i + 1)
-            finish(i)
-            if i + VE_BANKS < len(tiles):
+            apply_gate(i)
+            if i < POOL_ADDS:
+                finish(i, nc.gpsimd, f"result{i}")
+            elif i > POOL_ADDS:
+                finish(i - 1, nc.vector, f"gate{i}")
+            if i + VE_BANKS <= last:
                 value(i + VE_BANKS)
+        finish(last, nc.vector, f"result{last}")

@@ -41,13 +41,13 @@ def tile_list_engram_tier_bsig_kernel(
             return t
 
         def load_weight(w, a, name):
-            t = keep.tile([P, PACK, N], F32, name=name, align_bytes=64)
+            t = keep.tile([P, PACK, N], F32, name=name, tag=name, align_bytes=64)
             rows = w[a * P * PACK : (a + 1) * P * PACK, :]
             nc.sync.dma_start(out=t[:], in_=rows.rearrange("(p j) n -> p j n", j=PACK))
             return t
 
         def load_rows(x, c, name):
-            t = keep.tile([P, J], F32, name=name, align_bytes=64)
+            t = keep.tile([P, J], F32, name=name, tag=name, align_bytes=64)
             nc.sync.dma_start(out=t[:], in_=x[c * P : (c + 1) * P, :])
             return t
 
@@ -59,6 +59,8 @@ def tile_list_engram_tier_bsig_kernel(
         nc.gpsimd.memset(strip[:], 0.0)
         ident = strip[:, (PACK - 1) * P : PACK * P]
         make_identity(nc, ident, nomemset=True)
+        warm = keep.tile([P, 1], F32, name="warm")
+        nc.scalar.activation(out=warm[:], in_=strip[:, 0:1], func=ACT.Sigmoid)
         eye = keep.tile([P, PACK, P, PACK], BF16, name="eye", tag="eye", align_bytes=64)
         for t in range(PACK):
             shifted = strip[:, (PACK - 1 - t) * P : (2 * PACK - 1 - t) * P]
@@ -86,49 +88,49 @@ def tile_list_engram_tier_bsig_kernel(
             st_sb.append(load_rows(st, c, f"st{c}"))
             res_sb.append(load_rows(res, c, f"res{c}"))
 
+        def quantize_into(codes, src, name):
+            scales = keep.tile([P, codes.shape[1]], U8, name=name + "_s", align_bytes=64)
+            nc.vector.quantize_mx(out=codes.bitcast(FP8X4), scales=scales[:], in_=src)
+            return codes, scales
+
         def quantize(src, name, slot):
             width = src.shape[1] // PACK
             codes = keep.tile([P, width], U32, name=name + "_c", tag=slot, align_bytes=64)
-            scales = keep.tile([P, width], U8, name=name + "_s", align_bytes=64)
-            nc.vector.quantize_mx(out=codes[:].bitcast(FP8X4), scales=scales[:], in_=src)
-            return codes, scales
+            return quantize_into(codes[:], src, name)
 
         eye_q = quantize(eye[:].rearrange("p t m i -> p (t m i)"), "eye_q", "eye_c")
 
-        picked = {}
+        def pick_words(a, dst):
+            nc.vector.tensor_copy(dst, words[a][:].bitcast(U32).indirect(offsets[:]))
+            return dst
 
-        def pick_words(a, slot):
-            picked[a] = keep.tile([P, J], U32, name=f"picked{a}", tag=slot, align_bytes=64)
-            nc.vector.tensor_copy(picked[a][:], words[a][:].bitcast(U32).indirect(offsets[:]))
+        first_picks = keep.tile([P, J + J // 4], U32, name="first_picks", tag="eye", align_bytes=64)
+        picked = [pick_words(0, first_picks[:, 0:J])]
+        picked_s = first_picks[:, J:].bitcast(U8)
+        nc.vector.tensor_copy(picked_s, scale_win[:].bitcast(U8).indirect(offsets[:]))
 
-        pick_words(0, "eye")
-        picked_s = keep.tile([P, J], U8, name="picked_s", tag="words0", align_bytes=64)
-        nc.vector.tensor_copy(picked_s[:], scale_win[:].bitcast(U8).indirect(offsets[:]))
+        def interleaved(t, run):
+            return t.rearrange("p (c i t) -> p c t i", i=run, t=PACK)
 
-        def by_fours_out(t):
-            return t.rearrange("p (c i t) -> p c t i", i=4, t=PACK)
+        def planes(t, run):
+            return t.rearrange("p t (c i) -> p c t i", i=run)
 
-        def by_fours_in(t):
-            return t.rearrange("p t (c i) -> p c t i", i=4)
-
-        def cast(raw, n0, n1, name):
-            g = keep.tile([P, (n1 - n0) * PACK], BF16, name=name, tag=name, align_bytes=64)
-            nc.scalar.copy(out=by_fours_out(g[:]), in_=by_fours_in(raw[:, :, n0:n1]))
-            return g
+        def cast(raw, n0, n1, dst):
+            nc.scalar.copy(out=interleaved(dst, 4), in_=planes(raw[:, :, n0:n1], 4))
+            return dst
 
         units = [(a, h) for a in range(PASSES) for h in range(2)]
-        wv_bf = [cast(wv_raw[a], h * HALF, (h + 1) * HALF, f"wv_bf{a}{h}") for a, h in units]
-        wk_bf0 = cast(wk_raw[0], 0, N, "wk_bf0")
-        wk_bf1 = [cast(wk_raw[1], h * HALF, (h + 1) * HALF, f"wk_bf1{h}") for h in range(2)]
+        wv_bf, wv_q, wv_r, left = {}, {}, {}, {}
 
-        wv_q, wv_r, left = {}, {}, {}
+        def cast_wv(u, dst):
+            a, h = units[u]
+            wv_bf[u] = cast(wv_raw[a], h * HALF, (h + 1) * HALF, dst)
 
         def quantize_hi(u, slot):
-            wv_q[u] = quantize(wv_bf[u][:], f"wv_q{u}", slot)
+            wv_q[u] = quantize(wv_bf[u], f"wv_q{u}", slot)
             left[u] = keep.tile([P, HALF * PACK], BF16, name=f"left{u}", tag=f"left{u}", align_bytes=64)
 
-        def leftover(u, cc):
-            a, h = units[u]
+        def decode(u, cc):
             bank = psum.tile([P, PACK, P], F32, name="aux", tag="aux", bufs=AUX_BANKS)
             cols = slice(cc * P, (cc + 1) * P)
             for t in range(PACK):
@@ -141,37 +143,49 @@ def tile_list_engram_tier_bsig_kernel(
                     start=True,
                     stop=True,
                 )
+            a, h = units[u]
             n0 = h * HALF + cc * P
+            return bank, wv_raw[a][:, :, n0 : n0 + P], left[u][:, cc * P * PACK : (cc + 1) * P * PACK]
+
+        def leftover(u, cc):
+            bank, raw, dst = decode(u, cc)
             nc.vector.tensor_tensor(
-                out=by_fours_out(left[u][:, cc * P * PACK : (cc + 1) * P * PACK]),
-                in0=by_fours_in(wv_raw[a][:, :, n0 : n0 + P]),
-                in1=by_fours_in(bank[:]),
-                op=ALU.subtract,
+                out=interleaved(dst, 2), in0=planes(raw, 2), in1=planes(bank[:], 2), op=ALU.subtract
             )
 
         def quantize_lo(u):
             wv_r[u] = quantize(left[u][:], f"wv_r{u}", f"wv_r{u}")
 
-        quantize_hi(0, "scale_win")
-        quantize_hi(1, "wv_q1")
-        pick_words(1, "wv_bf01")
+        for u in range(len(units)):
+            rounded = keep.tile([P, HALF * PACK], BF16, name=f"wv_bf{u}", tag=f"wv_bf{u}", align_bytes=64)
+            cast_wv(u, rounded[:])
+        wk_bf = keep.tile([P, PASSES, N * PACK], BF16, name="wk_bf", align_bytes=64)
+        wk_bf0 = cast(wk_raw[0], 0, N, wk_bf[:, 0, :])
+        wk_bf1 = [
+            cast(wk_raw[1], h * HALF, (h + 1) * HALF, wk_bf[:, 1, h * HALF * PACK : (h + 1) * HALF * PACK])
+            for h in range(2)
+        ]
+        quantize_hi(0, "words0")
+        second_picks = keep.tile([P, J], U32, name="second_picks", tag="scale_win", align_bytes=64)
+        picked.append(pick_words(1, second_picks[:]))
+        quantize_hi(1, "wv_bf0")
         leftover(0, 0)
         leftover(0, 1)
         leftover(1, 0)
-        quantize_hi(2, "words1")
         quantize_lo(0)
         leftover(1, 1)
-        quantize_hi(3, "left0")
-        leftover(2, 0)
+        quantize_hi(2, "left0")
         quantize_lo(1)
+        leftover(2, 0)
+        quantize_hi(3, "left1")
         leftover(2, 1)
-        wk_q0 = quantize(wk_bf0[:], "wk_q0", "left1")
         leftover(3, 0)
         quantize_lo(2)
+        wk_codes = keep.tile([P, N + HALF], U32, name="wk_codes", tag="wv_bf3", align_bytes=64)
+        wk_q0 = quantize_into(wk_codes[:, 0:N], wk_bf0, "wk_q0")
+        wk_q1 = [quantize_into(wk_codes[:, N:], wk_bf1[0], "wk_q10")]
         leftover(3, 1)
-        wk_q1 = [quantize(wk_bf1[0][:], "wk_q10", "left2")]
         quantize_lo(3)
-        wk_q1.append(quantize(wk_bf1[1][:], "wk_q11", "left3"))
 
         def product(bank, parts, jh):
             js = slice(jh * JT, (jh + 1) * JT)
@@ -220,11 +234,13 @@ def tile_list_engram_tier_bsig_kernel(
             nc.sync.dma_start(out=out[c * P : (c + 1) * P, js], in_=result[:])
 
         last = len(tiles) - 1
+        make_gate(0)
+        make_gate(1)
+        wk_q1.append(quantize(wk_bf1[1], "wk_q11", "st0"))
         for i in range(VE_BANKS):
             value(i)
-        make_gate(0)
         for i in range(len(tiles)):
-            if i < last:
+            if 0 < i < last:
                 make_gate(i + 1)
             apply_gate(i)
             if i < POOL_ADDS:

from contextlib import ExitStack

import concourse.mybir as mybir
from concourse.masks import make_identity

K, N, T, J = 1024, 512, 2048, 1024
FLOPS = 3758096384

F32 = mybir.dt.float32
BF16 = mybir.dt.bfloat16
I32 = mybir.dt.int32
U32 = mybir.dt.uint32
U16 = mybir.dt.uint16
U8 = mybir.dt.uint8
FP8X4 = mybir.dt.float8_e4m3fn_x4
ALU = mybir.AluOpType
ACT = mybir.ActivationFunctionType

P = 128
PACK = 4
PASSES = K // (P * PACK)
HALF = N // 2
JT = 512
VE_BANKS = 5
AUX_BANKS = 3
POOL_ADDS = 5


def tile_list_engram_tier_bsig_kernel(
    tc, tab_words, tab_scales, wk, wv, st, b, res, offs, out
):
    nc = tc.nc
    with ExitStack() as ctx:
        keep = ctx.enter_context(tc.tile_pool(name="keep", bufs=1))
        work = ctx.enter_context(tc.tile_pool(name="work", bufs=8))
        psum = ctx.enter_context(tc.psum_pool(name="psum", bufs=1))

        def load_words(a):
            t = keep.tile([P, T], I32, name=f"words{a}", tag=f"words{a}", align_bytes=64)
            nc.sync.dma_start(out=t[:], in_=tab_words[a].rearrange("p t i -> p (t i)").bitcast(I32))
            return t

        def load_weight(w, a, name):
            t = keep.tile([P, PACK, N], F32, name=name, tag=name, align_bytes=64)
            rows = w[a * P * PACK : (a + 1) * P * PACK, :]
            nc.sync.dma_start(out=t[:], in_=rows.rearrange("(p j) n -> p j n", j=PACK))
            return t

        def load_rows(x, c, name):
            t = keep.tile([P, J], F32, name=name, tag=name, align_bytes=64)
            nc.sync.dma_start(out=t[:], in_=x[c * P : (c + 1) * P, :])
            return t

        scale_win = keep.tile([P, T // 4], I32, name="scale_win", tag="scale_win", align_bytes=64)
        nc.vector.memset(scale_win[:], 0)
        bias_rows = keep.tile([P, P], F32, name="bias_rows")
        nc.gpsimd.memset(bias_rows[:], 0.0)
        strip = keep.tile([P, (2 * PACK - 1) * P], F32, name="strip", align_bytes=64)
        nc.gpsimd.memset(strip[:], 0.0)
        ident = strip[:, (PACK - 1) * P : PACK * P]
        make_identity(nc, ident, nomemset=True)
        warm = keep.tile([P, 1], F32, name="warm")
        nc.scalar.activation(out=warm[:], in_=strip[:, 0:1], func=ACT.Sigmoid)
        eye = keep.tile([P, PACK, P, PACK], BF16, name="eye", tag="eye", align_bytes=64)
        for t in range(PACK):
            shifted = strip[:, (PACK - 1 - t) * P : (2 * PACK - 1 - t) * P]
            nc.vector.tensor_copy(out=eye[:, t, :, :], in_=shifted.rearrange("p (i m) -> p m i", i=PACK))

        words = [load_words(0)]
        offsets = keep.tile([P, J // 16], U16, name="offsets")
        nc.sync.dma_start(offsets[:], offs)
        for q in range(4):
            nc.sync.dma_start(
                out=scale_win[32 * q : 32 * q + 4 * PASSES, :],
                in_=tab_scales[:, 4 * q : 4 * q + 4, :].bitcast(I32),
            )
        nc.sync.dma_start(out=bias_rows[0 : N // P, :], in_=b.rearrange("(c p) -> c p", p=P))
        wv_raw = [load_weight(wv, 0, "wv_raw0")]
        words.append(load_words(1))
        wv_raw.append(load_weight(wv, 1, "wv_raw1"))
        wk_raw = [load_weight(wk, a, f"wk_raw{a}") for a in range(PASSES)]
        bias_bank = psum.tile([P, P], F32, name="aux", tag="aux", bufs=AUX_BANKS)
        nc.tensor.transpose(bias_bank[:], bias_rows[:], ident)
        bias = keep.tile([P, N // P], F32, name="bias")
        nc.scalar.copy(out=bias[:], in_=bias_bank[:, 0 : N // P])
        st_sb, res_sb = [], []
        for c in range(N // P):
            st_sb.append(load_rows(st, c, f"st{c}"))
            res_sb.append(load_rows(res, c, f"res{c}"))

        def quantize_into(codes, src, name):
            scales = keep.tile([P, codes.shape[1]], U8, name=name + "_s", align_bytes=64)
            nc.vector.quantize_mx(out=codes.bitcast(FP8X4), scales=scales[:], in_=src)
            return codes, scales

        def quantize(src, name, slot):
            width = src.shape[1] // PACK
            codes = keep.tile([P, width], U32, name=name + "_c", tag=slot, align_bytes=64)
            return quantize_into(codes[:], src, name)

        eye_q = quantize(eye[:].rearrange("p t m i -> p (t m i)"), "eye_q", "eye_c")

        def pick_words(a, dst):
            nc.vector.tensor_copy(dst, words[a][:].bitcast(U32).indirect(offsets[:]))
            return dst

        first_picks = keep.tile([P, J + J // 4], U32, name="first_picks", tag="eye", align_bytes=64)
        picked = [pick_words(0, first_picks[:, 0:J])]
        picked_s = first_picks[:, J:].bitcast(U8)
        nc.vector.tensor_copy(picked_s, scale_win[:].bitcast(U8).indirect(offsets[:]))

        def interleaved(t, run):
            return t.rearrange("p (c i t) -> p c t i", i=run, t=PACK)

        def planes(t, run):
            return t.rearrange("p t (c i) -> p c t i", i=run)

        def cast(raw, n0, n1, dst):
            nc.scalar.copy(out=interleaved(dst, 4), in_=planes(raw[:, :, n0:n1], 4))
            return dst

        units = [(a, h) for a in range(PASSES) for h in range(2)]
        wv_bf, wv_q, wv_r, left = {}, {}, {}, {}

        def cast_wv(u, dst):
            a, h = units[u]
            wv_bf[u] = cast(wv_raw[a], h * HALF, (h + 1) * HALF, dst)

        def quantize_hi(u, slot):
            wv_q[u] = quantize(wv_bf[u], f"wv_q{u}", slot)
            left[u] = keep.tile([P, HALF * PACK], BF16, name=f"left{u}", tag=f"left{u}", align_bytes=64)

        def decode(u, cc):
            bank = psum.tile([P, PACK, P], F32, name="aux", tag="aux", bufs=AUX_BANKS)
            cols = slice(cc * P, (cc + 1) * P)
            for t in range(PACK):
                nc.tensor.matmul_mx(
                    out=bank[:, t, :],
                    lhsT=eye_q[0][:, t * P : (t + 1) * P].bitcast(FP8X4),
                    lhsT_scale=eye_q[1][:, t * P : (t + 1) * P],
                    rhs=wv_q[u][0][:, cols].bitcast(FP8X4),
                    rhs_scale=wv_q[u][1][:, cols],
                    start=True,
                    stop=True,
                )
            a, h = units[u]
            n0 = h * HALF + cc * P
            return bank, wv_raw[a][:, :, n0 : n0 + P], left[u][:, cc * P * PACK : (cc + 1) * P * PACK]

        def leftover(u, cc):
            bank, raw, dst = decode(u, cc)
            nc.vector.tensor_tensor(
                out=interleaved(dst, 2), in0=planes(raw, 2), in1=planes(bank[:], 2), op=ALU.subtract
            )

        def quantize_lo(u):
            wv_r[u] = quantize(left[u][:], f"wv_r{u}", f"wv_r{u}")

        for u in range(len(units)):
            rounded = keep.tile([P, HALF * PACK], BF16, name=f"wv_bf{u}", tag=f"wv_bf{u}", align_bytes=64)
            cast_wv(u, rounded[:])
        wk_bf = keep.tile([P, PASSES, N * PACK], BF16, name="wk_bf", align_bytes=64)
        wk_bf0 = cast(wk_raw[0], 0, N, wk_bf[:, 0, :])
        wk_bf1 = [
            cast(wk_raw[1], h * HALF, (h + 1) * HALF, wk_bf[:, 1, h * HALF * PACK : (h + 1) * HALF * PACK])
            for h in range(2)
        ]
        quantize_hi(0, "words0")
        second_picks = keep.tile([P, J], U32, name="second_picks", tag="scale_win", align_bytes=64)
        picked.append(pick_words(1, second_picks[:]))
        quantize_hi(1, "wv_bf0")
        leftover(0, 0)
        leftover(0, 1)
        leftover(1, 0)
        quantize_lo(0)
        leftover(1, 1)
        quantize_hi(2, "left0")
        quantize_lo(1)
        leftover(2, 0)
        quantize_hi(3, "left1")
        leftover(2, 1)
        leftover(3, 0)
        quantize_lo(2)
        wk_codes = keep.tile([P, N + HALF], U32, name="wk_codes", tag="wv_bf3", align_bytes=64)
        wk_q0 = quantize_into(wk_codes[:, 0:N], wk_bf0, "wk_q0")
        wk_q1 = [quantize_into(wk_codes[:, N:], wk_bf1[0], "wk_q10")]
        leftover(3, 1)
        quantize_lo(3)

        def product(bank, parts, jh):
            js = slice(jh * JT, (jh + 1) * JT)
            for i, (pair, m0, a) in enumerate(parts):
                nc.tensor.matmul_mx(
                    out=bank[:],
                    lhsT=pair[0][:, m0 : m0 + P].bitcast(FP8X4),
                    lhsT_scale=pair[1][:, m0 : m0 + P],
                    rhs=picked[a][:, js].bitcast(FP8X4),
                    rhs_scale=picked_s[4 * a :, js],
                    start=(i == 0),
                    stop=(i == len(parts) - 1),
                )

        tiles = [(c, jh) for c in range(N // P) for jh in range(J // JT)]
        ve, gate, gated = {}, {}, {}

        def value(i):
            c, jh = tiles[i]
            h, m0 = c // 2, (c % 2) * P
            ve[i] = psum.tile([P, JT], F32, name="ve", tag="ve", bufs=VE_BANKS)
            parts = [(wv_q[h], m0, 0), (wv_r[h], m0, 0), (wv_q[2 + h], m0, 1), (wv_r[2 + h], m0, 1)]
            product(ve[i], parts, jh)

        def make_gate(i):
            c, jh = tiles[i]
            h, m0 = c // 2, (c % 2) * P
            ke = psum.tile([P, JT], F32, name="aux", tag="aux", bufs=AUX_BANKS)
            product(ke, [(wk_q0, c * P, 0), (wk_q1[h], m0, 1)], jh)
            logit = work.tile([P, JT], F32, name="logit")
            nc.vector.tensor_tensor(
                out=logit[:], in0=st_sb[c][:, jh * JT : (jh + 1) * JT], in1=ke[:], op=ALU.mult
            )
            gate[i] = keep.tile([P, JT], F32, name=f"gate{i}", tag=f"gate{i}")
            nc.scalar.activation(out=gate[i][:], in_=logit[:], func=ACT.Sigmoid, bias=bias[:, c : c + 1])

        def apply_gate(i):
            gated[i] = work.tile([P, JT], F32, name="gated")
            nc.vector.tensor_tensor(out=gated[i][:], in0=gate[i][:], in1=ve[i][:], op=ALU.mult)

        def finish(i, adder, slot):
            c, jh = tiles[i]
            js = slice(jh * JT, (jh + 1) * JT)
            result = keep.tile([P, JT], F32, name=f"result{i}", tag=slot)
            adder.tensor_tensor(out=result[:], in0=gated[i][:], in1=res_sb[c][:, js], op=ALU.add)
            nc.sync.dma_start(out=out[c * P : (c + 1) * P, js], in_=result[:])

        last = len(tiles) - 1
        make_gate(0)
        make_gate(1)
        wk_q1.append(quantize(wk_bf1[1], "wk_q11", "st0"))
        for i in range(VE_BANKS):
            value(i)
        for i in range(len(tiles)):
            if 0 < i < last:
                make_gate(i + 1)
            apply_gate(i)
            if i < POOL_ADDS:
                finish(i, nc.gpsimd, f"result{i}")
            elif i > POOL_ADDS:
                finish(i - 1, nc.vector, f"gate{i}")
            if i + VE_BANKS <= last:
                value(i + VE_BANKS)
        finish(last, nc.vector, f"result{last}")
